import numpy as np
import ml_dtypes


def mxq(x, axis, fmt="e4m3"):
    dtype, down = {"e4m3": (ml_dtypes.float8_e4m3fn, 7), "e5m2": (ml_dtypes.float8_e5m2, 14)}[fmt]
    v = np.moveaxis(np.asarray(x, np.float32).astype(ml_dtypes.bfloat16).astype(np.float64), axis, -1)
    blocks = v.reshape(v.shape[:-1] + (-1, 32))
    amax = np.abs(blocks).max(-1, keepdims=True)
    byte = np.maximum(np.where(amax > 0, np.frexp(amax)[1] - 1 + 127, 0) - down, 1)
    scale = np.exp2(byte - 127.0)
    codes = (blocks / scale).astype(np.float32).astype(dtype).astype(np.float64)
    return np.moveaxis((codes * scale).reshape(v.shape), -1, axis)


WIDE = False


def mx_kscale(k):
    if not WIDE:
        return np.ones(k)
    levels = np.array([10, -10, 5, -5, 0])
    if k % 512:
        return np.exp2(np.random.permutation(np.resize(levels, k // 32))).repeat(32)
    a = np.empty((k // 512, 16))
    for p in range(k // 512):
        a[p, :8] = np.random.permutation(np.resize(levels, 8))
        for g in range(8):
            far = levels[np.abs(levels - a[p, g]) >= 10]
            a[p, g + 8] = far[np.random.randint(len(far))]
    return np.exp2(a.ravel()).repeat(32)


def f64(x):
    return np.asarray(x).astype(np.float64)


def striped(idx):
    return np.tile(np.asarray(idx).reshape(-1, 16).T, (8, 1)).astype(np.uint16)


def unstriped(offs):
    return offs[:16].T.reshape(-1).astype(np.int64)


E2M1 = np.array([0.0, 0.5, 1.0, 1.5, 2.0, 3.0, 4.0, 6.0, -0.0, -0.5, -1.0, -1.5, -2.0, -3.0, -4.0, -6.0])


def pack_weight(w, fmt):
    k, n = w.shape
    w = f64(np.asarray(w, np.float32).astype(ml_dtypes.bfloat16)).reshape(k // 32, 32, n)
    amax = np.abs(w).max(1)
    if fmt == "e4m3":
        byte = np.frexp(amax)[1] - 1 + 127 - 7
    else:
        mant, ex = np.frexp(amax / 6.0)
        byte = np.where(mant > 0.5, ex, ex - 1) + 127
    byte = np.clip(np.where(amax > 0, byte, 1), 1, 254)
    scaled = (w * np.exp2(127.0 - byte)[:, None, :]).reshape(k, n).astype(np.float32)
    by_word = np.ascontiguousarray(scaled.reshape(k // 512, 128, 4, n).transpose(0, 1, 3, 2))
    if fmt == "e4m3":
        words = by_word.astype(ml_dtypes.float8_e4m3fn).view(np.uint8)
    else:
        c = by_word.astype(ml_dtypes.float4_e2m1fn).view(np.uint8) & 0xF
        words = (c[..., 0::2] | (c[..., 1::2] << 4)).reshape(k // 512, 128, 2 * n)
    return np.ascontiguousarray(words), np.ascontiguousarray(byte.astype(np.uint8).reshape(k // 512, 16, n))


def unpack_weight(words, scales, fmt):
    g, _, n = scales.shape
    words = np.ascontiguousarray(words).reshape(g, 128, n, -1)
    if fmt == "e4m3":
        vals = words.view(ml_dtypes.float8_e4m3fn).astype(np.float64)
    else:
        nib = np.empty((g, 128, n, 4), np.uint8)
        nib[..., 0::2] = words & 0xF
        nib[..., 1::2] = words >> 4
        vals = E2M1[nib]
    vals = vals * np.repeat(np.exp2(scales.astype(np.float64) - 127.0), 8, axis=1)[..., None]
    return vals.transpose(0, 1, 3, 2).reshape(g * 512, n)


def sigmoid(v):
    return 1.0 / (1.0 + np.exp(-v))


K, R, F, T, J, G = 512, 128, 512, 2048, 512, 32


def setup_inputs():
    n = np.random.standard_normal
    idx = np.random.permutation(T)[:J]
    fk = mx_kscale(K)
    ff = mx_kscale(F)
    tabp = pack_weight(n((K, T)) / fk[:, None], "e4m3")
    dtabp = pack_weight(n((K, T)) / fk[:, None], "e4m3")
    return {
        "tab_words": tabp[0],
        "tab_scales": tabp[1],
        "w1": (n((K, R)) * 1 / np.sqrt(K) * fk[:, None]).astype(np.float32),
        "steep": (np.random.uniform(1.0, 4.0, (R, 1))).astype(np.float32),
        "bias": (np.random.uniform(-0.5, 0.5, (R, 1))).astype(np.float32),
        "wo": (n((F, R)) * 1 / np.sqrt(F) * ff[:, None]).astype(np.float32),
        "dy": (n((F, J)) / ff[:, None]).astype(np.float32),
        "dtab_words": dtabp[0],
        "dtab_scales": dtabp[1],
        "og": (np.random.uniform(0.7, 2.0, (R, 1))).astype(np.float32),
        "base": (0.3 * n((R, J))).astype(np.float32),
        "offs": striped(idx),
    }


def reference(tab_words, tab_scales, w1, steep, bias, wo, dy, dtab_words, dtab_scales, og, base, offs):
    idx = unstriped(offs)
    tabu = unpack_weight(tab_words, tab_scales, "e4m3")
    dtabu = unpack_weight(dtab_words, dtab_scales, "e4m3")
    w1q = mxq(f64(w1), 0, "e4m3")
    tabidxg = tabu[:, idx]
    a = w1q.T @ tabidxg
    dtabidxg = dtabu[:, idx]
    ta = w1q.T @ dtabidxg
    m1 = a.reshape(R, G, J // G).mean(axis=2)
    gt = sigmoid(m1 * f64(steep) + f64(bias))
    woq = mxq(f64(wo), 0, "e4m3")
    dyq = mxq(f64(dy), 0, "e4m3")
    c0 = woq.T @ dyq
    dgr0 = c0 * a
    dgt = dgr0.reshape(R, G, J // G).sum(axis=2)
    xm1 = ta.reshape(R, G, J // G).mean(axis=2)
    xgt = xm1 * f64(steep) * gt * (1.0 - gt)
    xgr0 = np.repeat(xgt, J // G, axis=1)
    xdgr0 = ta * c0
    xdgt = xdgr0.reshape(R, G, J // G).sum(axis=2)
    xdm1 = ((xdgt * gt + xgt * dgt) * (1.0 - gt) + xgt * (-1.0) * dgt * gt) * f64(steep)
    xe1 = xdm1 / 16.0
    xr1 = np.repeat(xe1, J // G, axis=1)
    xda = xgr0 * c0 + xr1
    y = xda * f64(og) + f64(base)
    return y

@@ -1,0 +1,187 @@
+from contextlib import ExitStack
+
+import concourse.mybir as mybir
+
+F32 = mybir.dt.float32
+BF16 = mybir.dt.bfloat16
+I32 = mybir.dt.int32
+U32 = mybir.dt.uint32
+U16 = mybir.dt.uint16
+U8 = mybir.dt.uint8
+FP8X4 = mybir.dt.float8_e4m3fn_x4
+ALU = mybir.AluOpType
+ACT = mybir.ActivationFunctionType
+AXIS_X = mybir.AxisListType.X
+
+P = 128
+PACK = 4
+R, T, J = 128, 2048, 512
+GROUP = 16
+G = J // GROUP
+HALF = J // 2
+HG = G // 2
+QUARTER = J // 4
+FLOPS = 3 * 2 * 512 * R * J
+
+
+def interleave_views(dst, src):
+    return (dst.rearrange("p (c i) t -> p c t i", i=4), src.rearrange("p t (c i) -> p c t i", i=4))
+
+
+def by_group(ap):
+    return ap.rearrange("p (g i) -> p g i", i=GROUP)
+
+
+def spread(ap):
+    return ap.unsqueeze(2).to_broadcast([P, ap.shape[1], GROUP])
+
+
+def tile_attend_hvsqueeze_kernel(tc, tab_words, tab_scales, w1, steep, bias, wo, dy, dtab_words, dtab_scales, og, base, offs, out):
+    nc = tc.nc
+    with ExitStack() as ctx:
+        keep = ctx.enter_context(tc.tile_pool(name="keep", bufs=1))
+        psum = ctx.enter_context(tc.psum_pool(name="psum", bufs=1))
+
+        offsets = keep.tile([P, J // 16], U16, name="offsets")
+        nc.sync.dma_start(offsets[:], offs)
+
+        w1_raw = keep.tile([P, PACK, R], F32, name="w1_raw", tag="buf_w1")
+        nc.sync.dma_start(out=w1_raw[:], in_=w1.rearrange("(p t) r -> p t r", t=PACK))
+        tab_w = keep.tile([P, T], I32, name="tab_w", tag="buf_tab")
+        nc.sync.dma_start(out=tab_w[:], in_=tab_words[0].rearrange("p n t -> p (n t)").bitcast(I32))
+        dtab_w = keep.tile([P, T], I32, name="dtab_w", tag="buf_dtab")
+        nc.sync.dma_start(out=dtab_w[:], in_=dtab_words[0].rearrange("p n t -> p (n t)").bitcast(I32))
+
+        tab_s = keep.tile([P, T], U8, name="tab_s", tag="buf_ts", align_bytes=64)
+        dtab_s = keep.tile([P, T], U8, name="dtab_s", tag="buf_ds", align_bytes=64)
+        nc.vector.memset(tab_s[:].bitcast(I32), 0)
+        nc.gpsimd.memset(dtab_s[:].bitcast(I32), 0)
+        for i in range(4):
+            nc.scalar.dma_start(out=tab_s[i:P:32, :].bitcast(I32), in_=tab_scales[0, i:16:4, :].bitcast(I32))
+        for i in range(4):
+            queue = nc.scalar if i < 2 else nc.gpsimd
+            queue.dma_start(out=dtab_s[4 + i : P : 32, :].bitcast(I32), in_=dtab_scales[0, i:16:4, :].bitcast(I32))
+
+        tab_gs = keep.tile([P, J], U8, name="tab_gs", align_bytes=64)
+        dtab_gs = keep.tile([P, J], U8, name="dtab_gs", align_bytes=64)
+        nc.vector.tensor_copy(tab_gs[:], tab_s[:].indirect(offsets[:]))
+
+        w1_bf = keep.tile([P, R, PACK], BF16, name="w1_bf", tag="buf_w1bf", align_bytes=64)
+        dst, src = interleave_views(w1_bf[:], w1_raw[:])
+        nc.vector.tensor_copy(out=dst, in_=src)
+        nc.vector.tensor_copy(dtab_gs[:], dtab_s[:].indirect(offsets[:]))
+        w1_q = keep.tile([P, R], U32, name="w1_q", align_bytes=64)
+        w1_s = keep.tile([P, R], U8, name="w1_s", align_bytes=64)
+        nc.vector.quantize_mx(out=w1_q[:].bitcast(FP8X4), scales=w1_s[:], in_=w1_bf[:].rearrange("p r t -> p (r t)"))
+
+        params = keep.tile([P, 24], F32, name="params", tag="buf_w1")
+        steep_c, bias_c, og_c = params[:, 0:1], params[:, 8:9], params[:, 16:17]
+        nc.gpsimd.dma_start(out=steep_c, in_=steep)
+        nc.gpsimd.dma_start(out=bias_c, in_=bias)
+        nc.gpsimd.dma_start(out=og_c, in_=og)
+        s16 = keep.tile([P, 1], F32, name="s16")
+        ns16 = keep.tile([P, 1], F32, name="ns16")
+        m2s16 = keep.tile([P, 1], F32, name="m2s16")
+        nbias = keep.tile([P, 1], F32, name="nbias")
+        ogs16 = keep.tile([P, 1], F32, name="ogs16")
+        nc.gpsimd.tensor_scalar(s16[:], steep_c, 1.0 / GROUP, 0.0, ALU.mult, ALU.add)
+        nc.gpsimd.tensor_scalar(ns16[:], steep_c, -1.0 / GROUP, 0.0, ALU.mult, ALU.add)
+        nc.gpsimd.tensor_scalar(m2s16[:], steep_c, -2.0 / GROUP, 0.0, ALU.mult, ALU.add)
+        nc.gpsimd.tensor_scalar(nbias[:], bias_c, -1.0, 0.0, ALU.mult, ALU.add)
+        nc.gpsimd.tensor_tensor(ogs16[:], og_c, s16[:], ALU.mult)
+
+        tab_gw = keep.tile([P, J], U32, name="tab_gw", tag="buf_ts", align_bytes=64)
+        dtab_gw = keep.tile([P, J], U32, name="dtab_gw", tag="buf_ds", align_bytes=64)
+        cols = [slice(h * HALF, (h + 1) * HALF) for h in range(2)]
+        grps = [slice(h * HG, (h + 1) * HG) for h in range(2)]
+        a_ps = [psum.tile([P, HALF], F32, name=f"a_ps{h}") for h in range(2)]
+        ta_ps = [psum.tile([P, HALF], F32, name=f"ta_ps{h}") for h in range(2)]
+        c_ps = [psum.tile([P, HALF], F32, name=f"c_ps{h}") for h in range(2)]
+
+        for h in range(2):
+            nc.vector.tensor_copy(tab_gw[:, cols[h]], tab_w[:].bitcast(U32).indirect(offsets[:, grps[h]]))
+            nc.tensor.matmul_mx(out=a_ps[h][:], lhsT=w1_q[:].bitcast(FP8X4), lhsT_scale=w1_s[:],
+                                rhs=tab_gw[:, cols[h]].bitcast(FP8X4), rhs_scale=tab_gs[:, cols[h]], start=True, stop=True)
+
+        dy_rows = dy.rearrange("(p t) j -> p t j", t=PACK)
+        dy_raw0 = keep.tile([P, PACK, HALF], F32, name="dy_raw0", tag="buf_w1bf", align_bytes=64)
+        nc.sync.dma_start(out=dy_raw0[:], in_=dy_rows[:, :, cols[0]])
+        wo_raw = keep.tile([P, PACK, R], F32, name="wo_raw", tag="buf_tab")
+        nc.sync.dma_start(out=wo_raw[:], in_=wo.rearrange("(p t) r -> p t r", t=PACK))
+        dy_raw1 = keep.tile([P, PACK, HALF], F32, name="dy_raw1", tag="buf_ts", align_bytes=64)
+        nc.sync.dma_start(out=dy_raw1[:], in_=dy_rows[:, :, cols[1]])
+        dy_raw = [dy_raw0, dy_raw1]
+
+        sum_a = keep.tile([P, G], F32, name="sum_a")
+        for h in range(2):
+            nc.vector.tensor_reduce(sum_a[:, grps[h]], by_group(a_ps[h][:]), AXIS_X, ALU.add)
+        gate = keep.tile([P, G], F32, name="gate")
+        rest = keep.tile([P, G], F32, name="rest")
+        bend = keep.tile([P, G], F32, name="bend")
+        slope = keep.tile([P, G], F32, name="slope")
+        nc.scalar.activation(gate[:], sum_a[:], ACT.Sigmoid, bias=bias_c, scale=s16[:])
+        nc.scalar.activation(rest[:], sum_a[:], ACT.Sigmoid, bias=nbias[:], scale=ns16[:])
+        nc.scalar.activation(bend[:], gate[:], ACT.Identity, bias=s16[:], scale=m2s16[:])
+
+        for h in range(2):
+            nc.vector.tensor_copy(dtab_gw[:, cols[h]], dtab_w[:].bitcast(U32).indirect(offsets[:, grps[h]]))
+            nc.tensor.matmul_mx(out=ta_ps[h][:], lhsT=w1_q[:].bitcast(FP8X4), lhsT_scale=w1_s[:],
+                                rhs=dtab_gw[:, cols[h]].bitcast(FP8X4), rhs_scale=dtab_gs[4:P, cols[h]], start=True, stop=True)
+        base_sb = keep.tile([P, J], F32, name="base_sb", tag="buf_dtab")
+        nc.sync.dma_start(out=base_sb[:], in_=base)
+        nc.vector.scalar_tensor_tensor(slope[:], gate[:], ogs16[:], rest[:], ALU.mult, ALU.mult)
+
+        dy_bf = [keep.tile([P, HALF, PACK], BF16, name=f"dy_bf{h}", align_bytes=64) for h in range(2)]
+        wo_bf = keep.tile([P, R, PACK], BF16, name="wo_bf", align_bytes=64)
+
+        def cast_dy(h):
+            dst, src = interleave_views(dy_bf[h][:], dy_raw[h][:])
+            nc.scalar.copy(out=dst, in_=src)
+
+        cast_dy(0)
+        dst, src = interleave_views(wo_bf[:], wo_raw[:])
+        nc.scalar.copy(out=dst, in_=src)
+        cast_dy(1)
+
+        sum_ta = keep.tile([P, G], F32, name="sum_ta")
+        beta = keep.tile([P, G], F32, name="beta")
+        gain = keep.tile([P, G], F32, name="gain")
+        bent = keep.tile([P, J], F32, name="bent")
+        mix = keep.tile([P, J], F32, name="mix")
+        for h in range(2):
+            nc.vector.tensor_reduce(sum_ta[:, grps[h]], by_group(ta_ps[h][:]), AXIS_X, ALU.add)
+        for h in range(2):
+            nc.vector.tensor_tensor(beta[:, grps[h]], sum_ta[:, grps[h]], bend[:, grps[h]], ALU.mult)
+        nc.vector.tensor_tensor(gain[:], sum_ta[:], slope[:], ALU.mult)
+        for h in range(2):
+            nc.vector.tensor_tensor(by_group(bent[:, cols[h]]), by_group(a_ps[h][:]), spread(beta[:, grps[h]]), ALU.mult)
+        for h in range(2):
+            nc.vector.tensor_tensor(mix[:, cols[h]], ta_ps[h][:], bent[:, cols[h]], ALU.add)
+
+        wo_q = keep.tile([P, R], U32, name="wo_q", align_bytes=64)
+        wo_s = keep.tile([P, R], U8, name="wo_s", align_bytes=64)
+        nc.vector.quantize_mx(out=wo_q[:].bitcast(FP8X4), scales=wo_s[:], in_=wo_bf[:].rearrange("p r t -> p (r t)"))
+        dy_q = keep.tile([P, J], U32, name="dy_q", align_bytes=64)
+        dy_s = keep.tile([P, J], U8, name="dy_s", align_bytes=64)
+        for h in range(2):
+            nc.vector.quantize_mx(out=dy_q[:, cols[h]].bitcast(FP8X4), scales=dy_s[:, cols[h]], in_=dy_bf[h][:].rearrange("p j t -> p (j t)"))
+            nc.tensor.matmul_mx(out=c_ps[h][:], lhsT=wo_q[:].bitcast(FP8X4), lhsT_scale=wo_s[:],
+                                rhs=dy_q[:, cols[h]].bitcast(FP8X4), rhs_scale=dy_s[:, cols[h]], start=True, stop=True)
+
+        direct = keep.tile([P, J], F32, name="direct")
+        based = keep.tile([P, J], F32, name="based")
+        prod = keep.tile([P, J], F32, name="prod")
+        sum_p = keep.tile([P, G], F32, name="sum_p")
+        shift = keep.tile([P, G], F32, name="shift")
+        result = keep.tile([P, J], F32, name="result")
+        for h in range(2):
+            nc.vector.tensor_tensor(by_group(direct[:, cols[h]]), by_group(c_ps[h][:]), spread(gain[:, grps[h]]), ALU.mult)
+            nc.gpsimd.tensor_tensor(based[:, cols[h]], direct[:, cols[h]], base_sb[:, cols[h]], ALU.add)
+            nc.vector.tensor_tensor(prod[:, cols[h]], c_ps[h][:], mix[:, cols[h]], ALU.mult)
+        for h in range(2):
+            nc.vector.tensor_reduce(sum_p[:, grps[h]], by_group(prod[:, cols[h]]), AXIS_X, ALU.add)
+        for h in range(2):
+            nc.vector.tensor_tensor(shift[:, grps[h]], sum_p[:, grps[h]], slope[:, grps[h]], ALU.mult)
+        for h in range(2):
+            nc.vector.tensor_tensor(by_group(result[:, cols[h]]), by_group(based[:, cols[h]]), spread(shift[:, grps[h]]), ALU.add)
+            nc.sync.dma_start(out=out[:, cols[h]], in_=result[:, cols[h]])

@@ -20,7 +20,6 @@ GROUP = 16
 G = J // GROUP
 HALF = J // 2
 HG = G // 2
-QUARTER = J // 4
 FLOPS = 3 * 2 * 512 * R * J
 
 
@@ -40,58 +39,62 @@ def tile_attend_hvsqueeze_kernel(tc, tab_words, tab_scales, w1, steep, bias, wo,
     nc = tc.nc
     with ExitStack() as ctx:
         keep = ctx.enter_context(tc.tile_pool(name="keep", bufs=1))
+        laid = ctx.enter_context(tc.tile_pool(name="laid", bufs=1))
         psum = ctx.enter_context(tc.psum_pool(name="psum", bufs=1))
+
+        def at(offset, shape, dtype, name):
+            return laid.tile(shape, dtype, name=name, offset=offset, align_bytes=64)
+
+        A, B = 0, 16384
 
         offsets = keep.tile([P, J // 16], U16, name="offsets")
         nc.sync.dma_start(offsets[:], offs)
 
-        w1_raw = keep.tile([P, PACK, R], F32, name="w1_raw", tag="buf_w1")
+        w1_raw = at(A, [P, PACK, R], F32, "w1_raw")
         nc.sync.dma_start(out=w1_raw[:], in_=w1.rearrange("(p t) r -> p t r", t=PACK))
         tab_w = keep.tile([P, T], I32, name="tab_w", tag="buf_tab")
         nc.sync.dma_start(out=tab_w[:], in_=tab_words[0].rearrange("p n t -> p (n t)").bitcast(I32))
-        dtab_w = keep.tile([P, T], I32, name="dtab_w", tag="buf_dtab")
-        nc.sync.dma_start(out=dtab_w[:], in_=dtab_words[0].rearrange("p n t -> p (n t)").bitcast(I32))
 
-        tab_s = keep.tile([P, T], U8, name="tab_s", tag="buf_ts", align_bytes=64)
-        dtab_s = keep.tile([P, T], U8, name="dtab_s", tag="buf_ds", align_bytes=64)
+        tab_s = at(B, [P, T], U8, "tab_s")
+        dtab_s = keep.tile([P, T], U8, name="dtab_s")
         nc.vector.memset(tab_s[:].bitcast(I32), 0)
         nc.gpsimd.memset(dtab_s[:].bitcast(I32), 0)
+        warm_in = keep.tile([P, 1], F32, name="warm_in")
+        warm_out = keep.tile([P, 1], F32, name="warm_out")
+        nc.vector.memset(warm_in[:], 0.0)
         for i in range(4):
             nc.scalar.dma_start(out=tab_s[i:P:32, :].bitcast(I32), in_=tab_scales[0, i:16:4, :].bitcast(I32))
         for i in range(4):
             queue = nc.scalar if i < 2 else nc.gpsimd
             queue.dma_start(out=dtab_s[4 + i : P : 32, :].bitcast(I32), in_=dtab_scales[0, i:16:4, :].bitcast(I32))
 
-        tab_gs = keep.tile([P, J], U8, name="tab_gs", align_bytes=64)
-        dtab_gs = keep.tile([P, J], U8, name="dtab_gs", align_bytes=64)
-        nc.vector.tensor_copy(tab_gs[:], tab_s[:].indirect(offsets[:]))
+        nc.scalar.activation(warm_out[:], warm_in[:], ACT.Sigmoid)
 
         w1_bf = keep.tile([P, R, PACK], BF16, name="w1_bf", tag="buf_w1bf", align_bytes=64)
         dst, src = interleave_views(w1_bf[:], w1_raw[:])
         nc.vector.tensor_copy(out=dst, in_=src)
+
+        dtab_w = at(A + 128, [P, T], I32, "dtab_w")
+        nc.sync.dma_start(out=dtab_w[:], in_=dtab_words[0].rearrange("p n t -> p (n t)").bitcast(I32))
+        steep_c = at(A, [P, 1], F32, "steep_c")
+        bias_c = at(A + 64, [P, 1], F32, "bias_c")
+        nc.gpsimd.dma_start(out=steep_c[:], in_=steep)
+        nc.gpsimd.dma_start(out=bias_c[:], in_=bias)
+        s16 = keep.tile([P, 1], F32, name="s16")
+        nc.gpsimd.tensor_scalar(s16[:], steep_c[:], 1.0 / GROUP, 0.0, ALU.mult, ALU.add)
+
+        tab_gs = keep.tile([P, J], U8, name="tab_gs", align_bytes=64)
+        dtab_gs = keep.tile([P, J], U8, name="dtab_gs", align_bytes=64)
+        nc.vector.tensor_copy(tab_gs[:], tab_s[:].indirect(offsets[:]))
         nc.vector.tensor_copy(dtab_gs[:], dtab_s[:].indirect(offsets[:]))
-        w1_q = keep.tile([P, R], U32, name="w1_q", align_bytes=64)
+        w1_q = at(B, [P, R], U32, "w1_q")
         w1_s = keep.tile([P, R], U8, name="w1_s", align_bytes=64)
         nc.vector.quantize_mx(out=w1_q[:].bitcast(FP8X4), scales=w1_s[:], in_=w1_bf[:].rearrange("p r t -> p (r t)"))
+        og_c = at(B + 512, [P, 1], F32, "og_c")
+        nc.gpsimd.dma_start(out=og_c[:], in_=og)
 
-        params = keep.tile([P, 24], F32, name="params", tag="buf_w1")
-        steep_c, bias_c, og_c = params[:, 0:1], params[:, 8:9], params[:, 16:17]
-        nc.gpsimd.dma_start(out=steep_c, in_=steep)
-        nc.gpsimd.dma_start(out=bias_c, in_=bias)
-        nc.gpsimd.dma_start(out=og_c, in_=og)
-        s16 = keep.tile([P, 1], F32, name="s16")
-        ns16 = keep.tile([P, 1], F32, name="ns16")
-        m2s16 = keep.tile([P, 1], F32, name="m2s16")
-        nbias = keep.tile([P, 1], F32, name="nbias")
-        ogs16 = keep.tile([P, 1], F32, name="ogs16")
-        nc.gpsimd.tensor_scalar(s16[:], steep_c, 1.0 / GROUP, 0.0, ALU.mult, ALU.add)
-        nc.gpsimd.tensor_scalar(ns16[:], steep_c, -1.0 / GROUP, 0.0, ALU.mult, ALU.add)
-        nc.gpsimd.tensor_scalar(m2s16[:], steep_c, -2.0 / GROUP, 0.0, ALU.mult, ALU.add)
-        nc.gpsimd.tensor_scalar(nbias[:], bias_c, -1.0, 0.0, ALU.mult, ALU.add)
-        nc.gpsimd.tensor_tensor(ogs16[:], og_c, s16[:], ALU.mult)
-
-        tab_gw = keep.tile([P, J], U32, name="tab_gw", tag="buf_ts", align_bytes=64)
-        dtab_gw = keep.tile([P, J], U32, name="dtab_gw", tag="buf_ds", align_bytes=64)
+        tab_gw = at(B + 1024, [P, J], U32, "tab_gw")
+        dtab_gw = keep.tile([P, J], U32, name="dtab_gw", align_bytes=64)
         cols = [slice(h * HALF, (h + 1) * HALF) for h in range(2)]
         grps = [slice(h * HG, (h + 1) * HG) for h in range(2)]
         a_ps = [psum.tile([P, HALF], F32, name=f"a_ps{h}") for h in range(2)]
@@ -108,65 +111,69 @@ def tile_attend_hvsqueeze_kernel(tc, tab_words, tab_scales, w1, steep, bias, wo,
         nc.sync.dma_start(out=dy_raw0[:], in_=dy_rows[:, :, cols[0]])
         wo_raw = keep.tile([P, PACK, R], F32, name="wo_raw", tag="buf_tab")
         nc.sync.dma_start(out=wo_raw[:], in_=wo.rearrange("(p t) r -> p t r", t=PACK))
-        dy_raw1 = keep.tile([P, PACK, HALF], F32, name="dy_raw1", tag="buf_ts", align_bytes=64)
+        dy_raw1 = at(B + 1024, [P, PACK, HALF], F32, "dy_raw1")
         nc.sync.dma_start(out=dy_raw1[:], in_=dy_rows[:, :, cols[1]])
         dy_raw = [dy_raw0, dy_raw1]
 
-        sum_a = keep.tile([P, G], F32, name="sum_a")
+        sum_a = keep.tile([P, G], F32, name="sum_a", tag="buf_bf", align_bytes=64)
         for h in range(2):
             nc.vector.tensor_reduce(sum_a[:, grps[h]], by_group(a_ps[h][:]), AXIS_X, ALU.add)
         gate = keep.tile([P, G], F32, name="gate")
         rest = keep.tile([P, G], F32, name="rest")
         bend = keep.tile([P, G], F32, name="bend")
+        gate_og = keep.tile([P, G], F32, name="gate_og")
         slope = keep.tile([P, G], F32, name="slope")
-        nc.scalar.activation(gate[:], sum_a[:], ACT.Sigmoid, bias=bias_c, scale=s16[:])
-        nc.scalar.activation(rest[:], sum_a[:], ACT.Sigmoid, bias=nbias[:], scale=ns16[:])
-        nc.scalar.activation(bend[:], gate[:], ACT.Identity, bias=s16[:], scale=m2s16[:])
+        nc.scalar.activation(gate[:], sum_a[:], ACT.Sigmoid, bias=bias_c[:], scale=s16[:])
+        nc.scalar.activation(bend[:], gate[:], ACT.Identity, bias=1.0, scale=-2.0)
+        nc.scalar.activation(rest[:], gate[:], ACT.Identity, bias=1.0, scale=-1.0)
+        nc.scalar.activation(gate_og[:], gate[:], ACT.Copy, scale=og_c[:])
 
         for h in range(2):
             nc.vector.tensor_copy(dtab_gw[:, cols[h]], dtab_w[:].bitcast(U32).indirect(offsets[:, grps[h]]))
             nc.tensor.matmul_mx(out=ta_ps[h][:], lhsT=w1_q[:].bitcast(FP8X4), lhsT_scale=w1_s[:],
                                 rhs=dtab_gw[:, cols[h]].bitcast(FP8X4), rhs_scale=dtab_gs[4:P, cols[h]], start=True, stop=True)
-        base_sb = keep.tile([P, J], F32, name="base_sb", tag="buf_dtab")
+        base_sb = at(A + 128, [P, J], F32, "base_sb")
         nc.sync.dma_start(out=base_sb[:], in_=base)
-        nc.vector.scalar_tensor_tensor(slope[:], gate[:], ogs16[:], rest[:], ALU.mult, ALU.mult)
 
-        dy_bf = [keep.tile([P, HALF, PACK], BF16, name=f"dy_bf{h}", align_bytes=64) for h in range(2)]
-        wo_bf = keep.tile([P, R, PACK], BF16, name="wo_bf", align_bytes=64)
-
-        def cast_dy(h):
-            dst, src = interleave_views(dy_bf[h][:], dy_raw[h][:])
+        rounded = keep.tile([P, J + R, PACK], BF16, name="rounded", tag="buf_bf", align_bytes=64)
+        dy_bf = [rounded[:, cols[h], :] for h in range(2)]
+        wo_bf = rounded[:, J:, :]
+        for dst_ap, src_tile in ((dy_bf[0], dy_raw[0]), (wo_bf, wo_raw), (dy_bf[1], dy_raw[1])):
+            dst, src = interleave_views(dst_ap, src_tile[:])
             nc.scalar.copy(out=dst, in_=src)
 
-        cast_dy(0)
-        dst, src = interleave_views(wo_bf[:], wo_raw[:])
-        nc.scalar.copy(out=dst, in_=src)
-        cast_dy(1)
-
         sum_ta = keep.tile([P, G], F32, name="sum_ta")
-        beta = keep.tile([P, G], F32, name="beta")
+        beta = keep.tile([P, G], F32, name="beta", tag="buf_q", align_bytes=64)
         gain = keep.tile([P, G], F32, name="gain")
         bent = keep.tile([P, J], F32, name="bent")
         mix = keep.tile([P, J], F32, name="mix")
         for h in range(2):
             nc.vector.tensor_reduce(sum_ta[:, grps[h]], by_group(ta_ps[h][:]), AXIS_X, ALU.add)
         for h in range(2):
-            nc.vector.tensor_tensor(beta[:, grps[h]], sum_ta[:, grps[h]], bend[:, grps[h]], ALU.mult)
-        nc.vector.tensor_tensor(gain[:], sum_ta[:], slope[:], ALU.mult)
+            nc.vector.scalar_tensor_tensor(beta[:, grps[h]], sum_ta[:, grps[h]], s16[:], bend[:, grps[h]], ALU.mult, ALU.mult)
+        nc.vector.scalar_tensor_tensor(slope[:], gate_og[:], s16[:], rest[:], ALU.mult, ALU.mult)
         for h in range(2):
             nc.vector.tensor_tensor(by_group(bent[:, cols[h]]), by_group(a_ps[h][:]), spread(beta[:, grps[h]]), ALU.mult)
+        nc.vector.tensor_tensor(gain[:], sum_ta[:], slope[:], ALU.mult)
         for h in range(2):
             nc.vector.tensor_tensor(mix[:, cols[h]], ta_ps[h][:], bent[:, cols[h]], ALU.add)
 
-        wo_q = keep.tile([P, R], U32, name="wo_q", align_bytes=64)
-        wo_s = keep.tile([P, R], U8, name="wo_s", align_bytes=64)
-        nc.vector.quantize_mx(out=wo_q[:].bitcast(FP8X4), scales=wo_s[:], in_=wo_bf[:].rearrange("p r t -> p (r t)"))
-        dy_q = keep.tile([P, J], U32, name="dy_q", align_bytes=64)
-        dy_s = keep.tile([P, J], U8, name="dy_s", align_bytes=64)
-        for h in range(2):
-            nc.vector.quantize_mx(out=dy_q[:, cols[h]].bitcast(FP8X4), scales=dy_s[:, cols[h]], in_=dy_bf[h][:].rearrange("p j t -> p (j t)"))
-            nc.tensor.matmul_mx(out=c_ps[h][:], lhsT=wo_q[:].bitcast(FP8X4), lhsT_scale=wo_s[:],
-                                rhs=dy_q[:, cols[h]].bitcast(FP8X4), rhs_scale=dy_s[:, cols[h]], start=True, stop=True)
+        codes = keep.tile([P, J + R], U32, name="codes", tag="buf_q", align_bytes=64)
+        code_s = keep.tile([P, J + R], U8, name="code_s", align_bytes=64)
+        wo_cols = slice(J, J + R)
+
+        def quantize(where):
+            nc.vector.quantize_mx(out=codes[:, where].bitcast(FP8X4), scales=code_s[:, where], in_=rounded[:, where, :].rearrange("p j t -> p (j t)"))
+
+        def last_layer(h):
+            nc.tensor.matmul_mx(out=c_ps[h][:], lhsT=codes[:, wo_cols].bitcast(FP8X4), lhsT_scale=code_s[:, wo_cols],
+                                rhs=codes[:, cols[h]].bitcast(FP8X4), rhs_scale=code_s[:, cols[h]], start=True, stop=True)
+
+        quantize(cols[0])
+        quantize(wo_cols)
+        last_layer(0)
+        quantize(cols[1])
+        last_layer(1)
 
         direct = keep.tile([P, J], F32, name="direct")
         based = keep.tile([P, J], F32, name="based")

@@ -45,15 +45,9 @@ def tile_attend_hvsqueeze_kernel(tc, tab_words, tab_scales, w1, steep, bias, wo,
         def at(offset, shape, dtype, name):
             return laid.tile(shape, dtype, name=name, offset=offset, align_bytes=64)
 
-        A, B = 0, 16384
-
-        offsets = keep.tile([P, J // 16], U16, name="offsets")
-        nc.sync.dma_start(offsets[:], offs)
-
-        w1_raw = at(A, [P, PACK, R], F32, "w1_raw")
-        nc.sync.dma_start(out=w1_raw[:], in_=w1.rearrange("(p t) r -> p t r", t=PACK))
-        tab_w = keep.tile([P, T], I32, name="tab_w", tag="buf_tab")
-        nc.sync.dma_start(out=tab_w[:], in_=tab_words[0].rearrange("p n t -> p (n t)").bitcast(I32))
+        B = 0
+        cols = [slice(h * HALF, (h + 1) * HALF) for h in range(2)]
+        grps = [slice(h * HG, (h + 1) * HG) for h in range(2)]
 
         tab_s = at(B, [P, T], U8, "tab_s")
         dtab_s = keep.tile([P, T], U8, name="dtab_s")
@@ -62,41 +56,54 @@ def tile_attend_hvsqueeze_kernel(tc, tab_words, tab_scales, w1, steep, bias, wo,
         warm_in = keep.tile([P, 1], F32, name="warm_in")
         warm_out = keep.tile([P, 1], F32, name="warm_out")
         nc.vector.memset(warm_in[:], 0.0)
+
+        offsets = keep.tile([P, J // 16], U16, name="offsets")
+        w1_raw = keep.tile([P, PACK, R], F32, name="w1_raw")
+        tab_w = keep.tile([P, T], I32, name="tab_w")
+        dtab_w = keep.tile([P, T], I32, name="dtab_w")
+        steep_c = keep.tile([P, 1], F32, name="steep_c")
+        bias_c = keep.tile([P, 1], F32, name="bias_c")
+        og_c = keep.tile([P, 1], F32, name="og_c")
+        dy_raw = [keep.tile([P, PACK, HALF], F32, name=f"dy_raw{h}", tag=f"dy_raw{h}") for h in range(2)]
+        wo_raw = keep.tile([P, PACK, R], F32, name="wo_raw")
+        base_sb = keep.tile([P, J], F32, name="base_sb")
+        dy_rows = dy.rearrange("(p t) j -> p t j", t=PACK)
+
+        def load_scale_rows(plane, first, scales, i, queue=nc.sync):
+            queue.dma_start(out=plane[first + i : P : 32, :].bitcast(I32), in_=scales[0, i:16:4, :].bitcast(I32))
+
+        nc.sync.dma_start(offsets[:], offs)
+        nc.sync.dma_start(out=w1_raw[:], in_=w1.rearrange("(p t) r -> p t r", t=PACK))
         for i in range(4):
-            nc.scalar.dma_start(out=tab_s[i:P:32, :].bitcast(I32), in_=tab_scales[0, i:16:4, :].bitcast(I32))
+            load_scale_rows(tab_s, 0, tab_scales, i, nc.scalar if i % 2 else nc.sync)
+        nc.sync.dma_start(out=tab_w[:], in_=tab_words[0].rearrange("p n t -> p (n t)").bitcast(I32))
         for i in range(4):
-            queue = nc.scalar if i < 2 else nc.gpsimd
-            queue.dma_start(out=dtab_s[4 + i : P : 32, :].bitcast(I32), in_=dtab_scales[0, i:16:4, :].bitcast(I32))
+            load_scale_rows(dtab_s, 4, dtab_scales, i)
+        nc.sync.dma_start(out=steep_c[:], in_=steep)
+        nc.sync.dma_start(out=bias_c[:], in_=bias)
+        nc.sync.dma_start(out=dtab_w[:], in_=dtab_words[0].rearrange("p n t -> p (n t)").bitcast(I32))
+        nc.sync.dma_start(out=og_c[:], in_=og)
+        nc.sync.dma_start(out=wo_raw[:], in_=wo.rearrange("(p t) r -> p t r", t=PACK))
+        nc.sync.dma_start(out=dy_raw[0][:], in_=dy_rows[:, :, cols[0]])
+        nc.sync.dma_start(out=dy_raw[1][:], in_=dy_rows[:, :, cols[1]])
+        nc.sync.dma_start(out=base_sb[:], in_=base)
 
         nc.scalar.activation(warm_out[:], warm_in[:], ACT.Sigmoid)
-
-        w1_bf = keep.tile([P, R, PACK], BF16, name="w1_bf", tag="buf_w1bf", align_bytes=64)
+        w1_bf = keep.tile([P, R, PACK], BF16, name="w1_bf", align_bytes=64)
         dst, src = interleave_views(w1_bf[:], w1_raw[:])
         nc.vector.tensor_copy(out=dst, in_=src)
-
-        dtab_w = at(A + 128, [P, T], I32, "dtab_w")
-        nc.sync.dma_start(out=dtab_w[:], in_=dtab_words[0].rearrange("p n t -> p (n t)").bitcast(I32))
-        steep_c = at(A, [P, 1], F32, "steep_c")
-        bias_c = at(A + 64, [P, 1], F32, "bias_c")
-        nc.gpsimd.dma_start(out=steep_c[:], in_=steep)
-        nc.gpsimd.dma_start(out=bias_c[:], in_=bias)
         s16 = keep.tile([P, 1], F32, name="s16")
-        nc.gpsimd.tensor_scalar(s16[:], steep_c[:], 1.0 / GROUP, 0.0, ALU.mult, ALU.add)
+        nc.scalar.activation(s16[:], steep_c[:], ACT.Copy, scale=1.0 / GROUP)
 
         tab_gs = keep.tile([P, J], U8, name="tab_gs", align_bytes=64)
         dtab_gs = keep.tile([P, J], U8, name="dtab_gs", align_bytes=64)
         nc.vector.tensor_copy(tab_gs[:], tab_s[:].indirect(offsets[:]))
-        nc.vector.tensor_copy(dtab_gs[:], dtab_s[:].indirect(offsets[:]))
         w1_q = at(B, [P, R], U32, "w1_q")
         w1_s = keep.tile([P, R], U8, name="w1_s", align_bytes=64)
         nc.vector.quantize_mx(out=w1_q[:].bitcast(FP8X4), scales=w1_s[:], in_=w1_bf[:].rearrange("p r t -> p (r t)"))
-        og_c = at(B + 512, [P, 1], F32, "og_c")
-        nc.gpsimd.dma_start(out=og_c[:], in_=og)
 
-        tab_gw = at(B + 1024, [P, J], U32, "tab_gw")
+        tab_gw = keep.tile([P, J], U32, name="tab_gw", align_bytes=64)
         dtab_gw = keep.tile([P, J], U32, name="dtab_gw", align_bytes=64)
-        cols = [slice(h * HALF, (h + 1) * HALF) for h in range(2)]
-        grps = [slice(h * HG, (h + 1) * HG) for h in range(2)]
         a_ps = [psum.tile([P, HALF], F32, name=f"a_ps{h}") for h in range(2)]
         ta_ps = [psum.tile([P, HALF], F32, name=f"ta_ps{h}") for h in range(2)]
         c_ps = [psum.tile([P, HALF], F32, name=f"c_ps{h}") for h in range(2)]
@@ -106,14 +113,7 @@ def tile_attend_hvsqueeze_kernel(tc, tab_words, tab_scales, w1, steep, bias, wo,
             nc.tensor.matmul_mx(out=a_ps[h][:], lhsT=w1_q[:].bitcast(FP8X4), lhsT_scale=w1_s[:],
                                 rhs=tab_gw[:, cols[h]].bitcast(FP8X4), rhs_scale=tab_gs[:, cols[h]], start=True, stop=True)
 
-        dy_rows = dy.rearrange("(p t) j -> p t j", t=PACK)
-        dy_raw0 = keep.tile([P, PACK, HALF], F32, name="dy_raw0", tag="buf_w1bf", align_bytes=64)
-        nc.sync.dma_start(out=dy_raw0[:], in_=dy_rows[:, :, cols[0]])
-        wo_raw = keep.tile([P, PACK, R], F32, name="wo_raw", tag="buf_tab")
-        nc.sync.dma_start(out=wo_raw[:], in_=wo.rearrange("(p t) r -> p t r", t=PACK))
-        dy_raw1 = at(B + 1024, [P, PACK, HALF], F32, "dy_raw1")
-        nc.sync.dma_start(out=dy_raw1[:], in_=dy_rows[:, :, cols[1]])
-        dy_raw = [dy_raw0, dy_raw1]
+        nc.vector.tensor_copy(dtab_gs[:], dtab_s[:].indirect(offsets[:]))
 
         sum_a = keep.tile([P, G], F32, name="sum_a", tag="buf_bf", align_bytes=64)
         for h in range(2):
@@ -132,52 +132,45 @@ def tile_attend_hvsqueeze_kernel(tc, tab_words, tab_scales, w1, steep, bias, wo,
             nc.vector.tensor_copy(dtab_gw[:, cols[h]], dtab_w[:].bitcast(U32).indirect(offsets[:, grps[h]]))
             nc.tensor.matmul_mx(out=ta_ps[h][:], lhsT=w1_q[:].bitcast(FP8X4), lhsT_scale=w1_s[:],
                                 rhs=dtab_gw[:, cols[h]].bitcast(FP8X4), rhs_scale=dtab_gs[4:P, cols[h]], start=True, stop=True)
-        base_sb = at(A + 128, [P, J], F32, "base_sb")
-        nc.sync.dma_start(out=base_sb[:], in_=base)
 
-        rounded = keep.tile([P, J + R, PACK], BF16, name="rounded", tag="buf_bf", align_bytes=64)
-        dy_bf = [rounded[:, cols[h], :] for h in range(2)]
-        wo_bf = rounded[:, J:, :]
-        for dst_ap, src_tile in ((dy_bf[0], dy_raw[0]), (wo_bf, wo_raw), (dy_bf[1], dy_raw[1])):
+        wo_bf = keep.tile([P, R, PACK], BF16, name="wo_bf", align_bytes=64)
+        dy_bf = keep.tile([P, J, PACK], BF16, name="dy_bf", tag="buf_bf", align_bytes=64)
+        for dst_ap, src_tile in ((wo_bf[:], wo_raw), (dy_bf[:, cols[0], :], dy_raw[0]), (dy_bf[:, cols[1], :], dy_raw[1])):
             dst, src = interleave_views(dst_ap, src_tile[:])
             nc.scalar.copy(out=dst, in_=src)
+        wo_q = keep.tile([P, R], U32, name="wo_q", align_bytes=64)
+        wo_s = keep.tile([P, R], U8, name="wo_s", align_bytes=64)
+        nc.vector.quantize_mx(out=wo_q[:].bitcast(FP8X4), scales=wo_s[:], in_=wo_bf[:].rearrange("p r t -> p (r t)"))
 
         sum_ta = keep.tile([P, G], F32, name="sum_ta")
-        beta = keep.tile([P, G], F32, name="beta", tag="buf_q", align_bytes=64)
+        beta = keep.tile([P, G], F32, name="beta")
         gain = keep.tile([P, G], F32, name="gain")
-        bent = keep.tile([P, J], F32, name="bent")
-        mix = keep.tile([P, J], F32, name="mix")
+        bent = keep.tile([P, J], F32, name="bent", tag="dy_raw0")
+        mix = keep.tile([P, J], F32, name="mix", tag="dy_raw1")
         for h in range(2):
             nc.vector.tensor_reduce(sum_ta[:, grps[h]], by_group(ta_ps[h][:]), AXIS_X, ALU.add)
-        for h in range(2):
-            nc.vector.scalar_tensor_tensor(beta[:, grps[h]], sum_ta[:, grps[h]], s16[:], bend[:, grps[h]], ALU.mult, ALU.mult)
+        nc.vector.scalar_tensor_tensor(beta[:, grps[0]], sum_ta[:, grps[0]], s16[:], bend[:, grps[0]], ALU.mult, ALU.mult)
         nc.vector.scalar_tensor_tensor(slope[:], gate_og[:], s16[:], rest[:], ALU.mult, ALU.mult)
+        nc.vector.scalar_tensor_tensor(beta[:, grps[1]], sum_ta[:, grps[1]], s16[:], bend[:, grps[1]], ALU.mult, ALU.mult)
+        nc.vector.tensor_tensor(gain[:], sum_ta[:], slope[:], ALU.mult)
+        dy_q = keep.tile([P, J], U32, name="dy_q", align_bytes=64)
+        dy_s = keep.tile([P, J], U8, name="dy_s", align_bytes=64)
+
+        def last_layer(h):
+            nc.vector.quantize_mx(out=dy_q[:, cols[h]].bitcast(FP8X4), scales=dy_s[:, cols[h]], in_=dy_bf[:, cols[h], :].rearrange("p j t -> p (j t)"))
+            nc.tensor.matmul_mx(out=c_ps[h][:], lhsT=wo_q[:].bitcast(FP8X4), lhsT_scale=wo_s[:],
+                                rhs=dy_q[:, cols[h]].bitcast(FP8X4), rhs_scale=dy_s[:, cols[h]], start=True, stop=True)
+
+        last_layer(0)
         for h in range(2):
             nc.vector.tensor_tensor(by_group(bent[:, cols[h]]), by_group(a_ps[h][:]), spread(beta[:, grps[h]]), ALU.mult)
-        nc.vector.tensor_tensor(gain[:], sum_ta[:], slope[:], ALU.mult)
+        last_layer(1)
         for h in range(2):
             nc.vector.tensor_tensor(mix[:, cols[h]], ta_ps[h][:], bent[:, cols[h]], ALU.add)
 
-        codes = keep.tile([P, J + R], U32, name="codes", tag="buf_q", align_bytes=64)
-        code_s = keep.tile([P, J + R], U8, name="code_s", align_bytes=64)
-        wo_cols = slice(J, J + R)
-
-        def quantize(where):
-            nc.vector.quantize_mx(out=codes[:, where].bitcast(FP8X4), scales=code_s[:, where], in_=rounded[:, where, :].rearrange("p j t -> p (j t)"))
-
-        def last_layer(h):
-            nc.tensor.matmul_mx(out=c_ps[h][:], lhsT=codes[:, wo_cols].bitcast(FP8X4), lhsT_scale=code_s[:, wo_cols],
-                                rhs=codes[:, cols[h]].bitcast(FP8X4), rhs_scale=code_s[:, cols[h]], start=True, stop=True)
-
-        quantize(cols[0])
-        quantize(wo_cols)
-        last_layer(0)
-        quantize(cols[1])
-        last_layer(1)
-
-        direct = keep.tile([P, J], F32, name="direct")
+        terms = keep.tile([P, 2 * J], F32, name="terms")
+        direct, prod = terms[:, :J], terms[:, J:]
         based = keep.tile([P, J], F32, name="based")
-        prod = keep.tile([P, J], F32, name="prod")
         sum_p = keep.tile([P, G], F32, name="sum_p")
         shift = keep.tile([P, G], F32, name="shift")
         result = keep.tile([P, J], F32, name="result")

@@ -52,7 +52,7 @@ def tile_attend_hvsqueeze_kernel(tc, tab_words, tab_scales, w1, steep, bias, wo,
         tab_s = at(B, [P, T], U8, "tab_s")
         dtab_s = keep.tile([P, T], U8, name="dtab_s")
         nc.vector.memset(tab_s[:].bitcast(I32), 0)
-        nc.gpsimd.memset(dtab_s[:].bitcast(I32), 0)
+        nc.vector.memset(dtab_s[:].bitcast(I32), 0)
         warm_in = keep.tile([P, 1], F32, name="warm_in")
         warm_out = keep.tile([P, 1], F32, name="warm_out")
         nc.vector.memset(warm_in[:], 0.0)
@@ -62,8 +62,8 @@ def tile_attend_hvsqueeze_kernel(tc, tab_words, tab_scales, w1, steep, bias, wo,
         tab_w = keep.tile([P, T], I32, name="tab_w")
         dtab_w = keep.tile([P, T], I32, name="dtab_w")
         steep_c = keep.tile([P, 1], F32, name="steep_c")
-        bias_c = keep.tile([P, 1], F32, name="bias_c")
-        og_c = keep.tile([P, 1], F32, name="og_c")
+        bias_c = keep.tile([P, 1], F32, name="bias_c", tag="dy_bf1", align_bytes=64)
+        og_c = keep.tile([P, 1], F32, name="og_c", tag="sums")
         dy_raw = [keep.tile([P, PACK, HALF], F32, name=f"dy_raw{h}", tag=f"dy_raw{h}") for h in range(2)]
         wo_raw = keep.tile([P, PACK, R], F32, name="wo_raw")
         base_sb = keep.tile([P, J], F32, name="base_sb")
@@ -79,12 +79,12 @@ def tile_attend_hvsqueeze_kernel(tc, tab_words, tab_scales, w1, steep, bias, wo,
         nc.sync.dma_start(out=tab_w[:], in_=tab_words[0].rearrange("p n t -> p (n t)").bitcast(I32))
         for i in range(4):
             load_scale_rows(dtab_s, 4, dtab_scales, i)
-        nc.sync.dma_start(out=steep_c[:], in_=steep)
-        nc.sync.dma_start(out=bias_c[:], in_=bias)
+        nc.gpsimd.dma_start(out=steep_c[:], in_=steep)
+        nc.gpsimd.dma_start(out=bias_c[:], in_=bias)
         nc.sync.dma_start(out=dtab_w[:], in_=dtab_words[0].rearrange("p n t -> p (n t)").bitcast(I32))
         nc.sync.dma_start(out=og_c[:], in_=og)
-        nc.sync.dma_start(out=wo_raw[:], in_=wo.rearrange("(p t) r -> p t r", t=PACK))
         nc.sync.dma_start(out=dy_raw[0][:], in_=dy_rows[:, :, cols[0]])
+        nc.sync.dma_start(out=wo_raw[:], in_=wo.rearrange("(p t) r -> p t r", t=PACK))
         nc.sync.dma_start(out=dy_raw[1][:], in_=dy_rows[:, :, cols[1]])
         nc.sync.dma_start(out=base_sb[:], in_=base)
 
@@ -103,70 +103,75 @@ def tile_attend_hvsqueeze_kernel(tc, tab_words, tab_scales, w1, steep, bias, wo,
         nc.vector.quantize_mx(out=w1_q[:].bitcast(FP8X4), scales=w1_s[:], in_=w1_bf[:].rearrange("p r t -> p (r t)"))
 
         tab_gw = keep.tile([P, J], U32, name="tab_gw", align_bytes=64)
-        dtab_gw = keep.tile([P, J], U32, name="dtab_gw", align_bytes=64)
-        a_ps = [psum.tile([P, HALF], F32, name=f"a_ps{h}") for h in range(2)]
+        dtab_gw = [keep.tile([P, HALF], U32, name=f"dtab_gw{h}", tag=f"dtab_gw{h}", align_bytes=64) for h in range(2)]
+        a_ps = psum.tile([P, J], F32, name="a_ps")
         ta_ps = [psum.tile([P, HALF], F32, name=f"ta_ps{h}") for h in range(2)]
         c_ps = [psum.tile([P, HALF], F32, name=f"c_ps{h}") for h in range(2)]
 
-        for h in range(2):
-            nc.vector.tensor_copy(tab_gw[:, cols[h]], tab_w[:].bitcast(U32).indirect(offsets[:, grps[h]]))
-            nc.tensor.matmul_mx(out=a_ps[h][:], lhsT=w1_q[:].bitcast(FP8X4), lhsT_scale=w1_s[:],
-                                rhs=tab_gw[:, cols[h]].bitcast(FP8X4), rhs_scale=tab_gs[:, cols[h]], start=True, stop=True)
+        nc.vector.tensor_copy(tab_gw[:], tab_w[:].bitcast(U32).indirect(offsets[:]))
+        nc.tensor.matmul_mx(out=a_ps[:], lhsT=w1_q[:].bitcast(FP8X4), lhsT_scale=w1_s[:],
+                            rhs=tab_gw[:].bitcast(FP8X4), rhs_scale=tab_gs[:], start=True, stop=True)
 
         nc.vector.tensor_copy(dtab_gs[:], dtab_s[:].indirect(offsets[:]))
+        a_sb = keep.tile([P, HALF], F32, name="a_sb")
+        nc.scalar.copy(out=a_sb[:], in_=a_ps[:, cols[1]])
+        ogs16 = keep.tile([P, 1], F32, name="ogs16")
+        nc.scalar.activation(ogs16[:], og_c[:], ACT.Copy, scale=s16[:])
 
-        sum_a = keep.tile([P, G], F32, name="sum_a", tag="buf_bf", align_bytes=64)
         for h in range(2):
-            nc.vector.tensor_reduce(sum_a[:, grps[h]], by_group(a_ps[h][:]), AXIS_X, ALU.add)
-        gate = keep.tile([P, G], F32, name="gate")
+            nc.vector.tensor_copy(dtab_gw[h][:], dtab_w[:].bitcast(U32).indirect(offsets[:, grps[h]]))
+            nc.tensor.matmul_mx(out=ta_ps[h][:], lhsT=w1_q[:].bitcast(FP8X4), lhsT_scale=w1_s[:],
+                                rhs=dtab_gw[h][:].bitcast(FP8X4), rhs_scale=dtab_gs[4:P, cols[h]], start=True, stop=True)
+
+        sums = keep.tile([P, 2 * G], F32, name="sums", tag="sums")
+        sum_a, sum_ta = sums[:, :G], sums[:, G:]
+        nc.vector.tensor_reduce(sum_a, by_group(a_ps[:]), AXIS_X, ALU.add)
+        dy_bf = []
+
+        def round_dy(h):
+            dy_bf.append(keep.tile([P, HALF, PACK], BF16, name=f"dy_bf{h}", tag=f"dy_bf{h}", align_bytes=64))
+            dst, src = interleave_views(dy_bf[h][:], dy_raw[h][:])
+            nc.scalar.copy(out=dst, in_=src)
+
+        round_dy(0)
+        gate = keep.tile([P, G], F32, name="gate", tag="dy_raw0")
         rest = keep.tile([P, G], F32, name="rest")
         bend = keep.tile([P, G], F32, name="bend")
-        gate_og = keep.tile([P, G], F32, name="gate_og")
         slope = keep.tile([P, G], F32, name="slope")
-        nc.scalar.activation(gate[:], sum_a[:], ACT.Sigmoid, bias=bias_c[:], scale=s16[:])
+        nc.scalar.activation(gate[:], sum_a, ACT.Sigmoid, bias=bias_c[:], scale=s16[:])
         nc.scalar.activation(bend[:], gate[:], ACT.Identity, bias=1.0, scale=-2.0)
         nc.scalar.activation(rest[:], gate[:], ACT.Identity, bias=1.0, scale=-1.0)
-        nc.scalar.activation(gate_og[:], gate[:], ACT.Copy, scale=og_c[:])
-
-        for h in range(2):
-            nc.vector.tensor_copy(dtab_gw[:, cols[h]], dtab_w[:].bitcast(U32).indirect(offsets[:, grps[h]]))
-            nc.tensor.matmul_mx(out=ta_ps[h][:], lhsT=w1_q[:].bitcast(FP8X4), lhsT_scale=w1_s[:],
-                                rhs=dtab_gw[:, cols[h]].bitcast(FP8X4), rhs_scale=dtab_gs[4:P, cols[h]], start=True, stop=True)
 
         wo_bf = keep.tile([P, R, PACK], BF16, name="wo_bf", align_bytes=64)
-        dy_bf = keep.tile([P, J, PACK], BF16, name="dy_bf", tag="buf_bf", align_bytes=64)
-        for dst_ap, src_tile in ((wo_bf[:], wo_raw), (dy_bf[:, cols[0], :], dy_raw[0]), (dy_bf[:, cols[1], :], dy_raw[1])):
-            dst, src = interleave_views(dst_ap, src_tile[:])
-            nc.scalar.copy(out=dst, in_=src)
-        wo_q = keep.tile([P, R], U32, name="wo_q", align_bytes=64)
+        round_dy(1)
+        nc.gpsimd.tensor_scalar(wo_bf[:], wo_raw[:].rearrange("p t r -> p r t"), 1.0, 0.0, ALU.mult, ALU.add)
+        codes = keep.tile([P, J + R], U32, name="codes", tag="dtab_gw1", align_bytes=64)
+        dy_q, wo_q = codes[:, :J], codes[:, J:]
         wo_s = keep.tile([P, R], U8, name="wo_s", align_bytes=64)
-        nc.vector.quantize_mx(out=wo_q[:].bitcast(FP8X4), scales=wo_s[:], in_=wo_bf[:].rearrange("p r t -> p (r t)"))
 
-        sum_ta = keep.tile([P, G], F32, name="sum_ta")
         beta = keep.tile([P, G], F32, name="beta")
         gain = keep.tile([P, G], F32, name="gain")
-        bent = keep.tile([P, J], F32, name="bent", tag="dy_raw0")
-        mix = keep.tile([P, J], F32, name="mix", tag="dy_raw1")
+        bent = keep.tile([P, J], F32, name="bent")
         for h in range(2):
             nc.vector.tensor_reduce(sum_ta[:, grps[h]], by_group(ta_ps[h][:]), AXIS_X, ALU.add)
-        nc.vector.scalar_tensor_tensor(beta[:, grps[0]], sum_ta[:, grps[0]], s16[:], bend[:, grps[0]], ALU.mult, ALU.mult)
-        nc.vector.scalar_tensor_tensor(slope[:], gate_og[:], s16[:], rest[:], ALU.mult, ALU.mult)
-        nc.vector.scalar_tensor_tensor(beta[:, grps[1]], sum_ta[:, grps[1]], s16[:], bend[:, grps[1]], ALU.mult, ALU.mult)
-        nc.vector.tensor_tensor(gain[:], sum_ta[:], slope[:], ALU.mult)
-        dy_q = keep.tile([P, J], U32, name="dy_q", align_bytes=64)
+        nc.vector.quantize_mx(out=wo_q.bitcast(FP8X4), scales=wo_s[:], in_=wo_bf[:].rearrange("p r t -> p (r t)"))
         dy_s = keep.tile([P, J], U8, name="dy_s", align_bytes=64)
 
         def last_layer(h):
-            nc.vector.quantize_mx(out=dy_q[:, cols[h]].bitcast(FP8X4), scales=dy_s[:, cols[h]], in_=dy_bf[:, cols[h], :].rearrange("p j t -> p (j t)"))
-            nc.tensor.matmul_mx(out=c_ps[h][:], lhsT=wo_q[:].bitcast(FP8X4), lhsT_scale=wo_s[:],
+            nc.vector.quantize_mx(out=dy_q[:, cols[h]].bitcast(FP8X4), scales=dy_s[:, cols[h]], in_=dy_bf[h][:].rearrange("p j t -> p (j t)"))
+            nc.tensor.matmul_mx(out=c_ps[h][:], lhsT=wo_q.bitcast(FP8X4), lhsT_scale=wo_s[:],
                                 rhs=dy_q[:, cols[h]].bitcast(FP8X4), rhs_scale=dy_s[:, cols[h]], start=True, stop=True)
 
         last_layer(0)
-        for h in range(2):
-            nc.vector.tensor_tensor(by_group(bent[:, cols[h]]), by_group(a_ps[h][:]), spread(beta[:, grps[h]]), ALU.mult)
+        nc.vector.scalar_tensor_tensor(slope[:], gate[:], ogs16[:], rest[:], ALU.mult, ALU.mult)
+        nc.vector.scalar_tensor_tensor(beta[:], sum_ta, s16[:], bend[:], ALU.mult, ALU.mult)
+        nc.vector.tensor_tensor(gain[:], sum_ta, slope[:], ALU.mult)
+        nc.gpsimd.tensor_tensor(by_group(bent[:, cols[1]]), by_group(a_sb[:]), spread(beta[:, grps[1]]), ALU.mult)
+        nc.vector.tensor_tensor(by_group(bent[:, cols[0]]), by_group(a_ps[:, cols[0]]), spread(beta[:, grps[0]]), ALU.mult)
+        mix = [keep.tile([P, HALF], F32, name="mix0"), keep.tile([P, HALF], F32, name="mix1", tag="dy_raw1")]
+        nc.vector.tensor_tensor(mix[0][:], ta_ps[0][:], bent[:, cols[0]], ALU.add)
         last_layer(1)
-        for h in range(2):
-            nc.vector.tensor_tensor(mix[:, cols[h]], ta_ps[h][:], bent[:, cols[h]], ALU.add)
+        nc.vector.tensor_tensor(mix[1][:], ta_ps[1][:], bent[:, cols[1]], ALU.add)
 
         terms = keep.tile([P, 2 * J], F32, name="terms")
         direct, prod = terms[:, :J], terms[:, J:]
@@ -177,7 +182,7 @@ def tile_attend_hvsqueeze_kernel(tc, tab_words, tab_scales, w1, steep, bias, wo,
         for h in range(2):
             nc.vector.tensor_tensor(by_group(direct[:, cols[h]]), by_group(c_ps[h][:]), spread(gain[:, grps[h]]), ALU.mult)
             nc.gpsimd.tensor_tensor(based[:, cols[h]], direct[:, cols[h]], base_sb[:, cols[h]], ALU.add)
-            nc.vector.tensor_tensor(prod[:, cols[h]], c_ps[h][:], mix[:, cols[h]], ALU.mult)
+            nc.vector.tensor_tensor(prod[:, cols[h]], c_ps[h][:], mix[h][:], ALU.mult)
         for h in range(2):
             nc.vector.tensor_reduce(sum_p[:, grps[h]], by_group(prod[:, cols[h]]), AXIS_X, ALU.add)
         for h in range(2):

from contextlib import ExitStack

import concourse.mybir as mybir

F32 = mybir.dt.float32
BF16 = mybir.dt.bfloat16
I32 = mybir.dt.int32
U32 = mybir.dt.uint32
U16 = mybir.dt.uint16
U8 = mybir.dt.uint8
FP8X4 = mybir.dt.float8_e4m3fn_x4
ALU = mybir.AluOpType
ACT = mybir.ActivationFunctionType
AXIS_X = mybir.AxisListType.X

P = 128
PACK = 4
R, T, J = 128, 2048, 512
GROUP = 16
G = J // GROUP
HALF = J // 2
HG = G // 2
FLOPS = 3 * 2 * 512 * R * J


def interleave_views(dst, src):
    return (dst.rearrange("p (c i) t -> p c t i", i=4), src.rearrange("p t (c i) -> p c t i", i=4))


def by_group(ap):
    return ap.rearrange("p (g i) -> p g i", i=GROUP)


def spread(ap):
    return ap.unsqueeze(2).to_broadcast([P, ap.shape[1], GROUP])


def tile_attend_hvsqueeze_kernel(tc, tab_words, tab_scales, w1, steep, bias, wo, dy, dtab_words, dtab_scales, og, base, offs, out):
    nc = tc.nc
    with ExitStack() as ctx:
        keep = ctx.enter_context(tc.tile_pool(name="keep", bufs=1))
        laid = ctx.enter_context(tc.tile_pool(name="laid", bufs=1))
        psum = ctx.enter_context(tc.psum_pool(name="psum", bufs=1))

        def at(offset, shape, dtype, name):
            return laid.tile(shape, dtype, name=name, offset=offset, align_bytes=64)

        B = 0
        cols = [slice(h * HALF, (h + 1) * HALF) for h in range(2)]
        grps = [slice(h * HG, (h + 1) * HG) for h in range(2)]

        tab_s = at(B, [P, T], U8, "tab_s")
        dtab_s = keep.tile([P, T], U8, name="dtab_s")
        nc.vector.memset(tab_s[:].bitcast(I32), 0)
        nc.vector.memset(dtab_s[:].bitcast(I32), 0)
        warm_in = keep.tile([P, 1], F32, name="warm_in")
        warm_out = keep.tile([P, 1], F32, name="warm_out")
        nc.vector.memset(warm_in[:], 0.0)

        offsets = keep.tile([P, J // 16], U16, name="offsets")
        w1_raw = keep.tile([P, PACK, R], F32, name="w1_raw")
        tab_w = keep.tile([P, T], I32, name="tab_w")
        dtab_w = keep.tile([P, T], I32, name="dtab_w")
        steep_c = keep.tile([P, 1], F32, name="steep_c")
        bias_c = keep.tile([P, 1], F32, name="bias_c", tag="dy_bf1", align_bytes=64)
        og_c = keep.tile([P, 1], F32, name="og_c", tag="sums")
        dy_raw = [keep.tile([P, PACK, HALF], F32, name=f"dy_raw{h}", tag=f"dy_raw{h}") for h in range(2)]
        wo_raw = keep.tile([P, PACK, R], F32, name="wo_raw")
        base_sb = keep.tile([P, J], F32, name="base_sb")
        dy_rows = dy.rearrange("(p t) j -> p t j", t=PACK)

        def load_scale_rows(plane, first, scales, i, queue=nc.sync):
            queue.dma_start(out=plane[first + i : P : 32, :].bitcast(I32), in_=scales[0, i:16:4, :].bitcast(I32))

        nc.sync.dma_start(offsets[:], offs)
        nc.sync.dma_start(out=w1_raw[:], in_=w1.rearrange("(p t) r -> p t r", t=PACK))
        for i in range(4):
            load_scale_rows(tab_s, 0, tab_scales, i, nc.scalar if i % 2 else nc.sync)
        nc.sync.dma_start(out=tab_w[:], in_=tab_words[0].rearrange("p n t -> p (n t)").bitcast(I32))
        for i in range(4):
            load_scale_rows(dtab_s, 4, dtab_scales, i)
        nc.gpsimd.dma_start(out=steep_c[:], in_=steep)
        nc.gpsimd.dma_start(out=bias_c[:], in_=bias)
        nc.sync.dma_start(out=dtab_w[:], in_=dtab_words[0].rearrange("p n t -> p (n t)").bitcast(I32))
        nc.sync.dma_start(out=og_c[:], in_=og)
        nc.sync.dma_start(out=dy_raw[0][:], in_=dy_rows[:, :, cols[0]])
        nc.sync.dma_start(out=wo_raw[:], in_=wo.rearrange("(p t) r -> p t r", t=PACK))
        nc.sync.dma_start(out=dy_raw[1][:], in_=dy_rows[:, :, cols[1]])
        nc.sync.dma_start(out=base_sb[:], in_=base)

        nc.scalar.activation(warm_out[:], warm_in[:], ACT.Sigmoid)
        w1_bf = keep.tile([P, R, PACK], BF16, name="w1_bf", align_bytes=64)
        dst, src = interleave_views(w1_bf[:], w1_raw[:])
        nc.vector.tensor_copy(out=dst, in_=src)
        s16 = keep.tile([P, 1], F32, name="s16")
        nc.scalar.activation(s16[:], steep_c[:], ACT.Copy, scale=1.0 / GROUP)

        tab_gs = keep.tile([P, J], U8, name="tab_gs", align_bytes=64)
        dtab_gs = keep.tile([P, J], U8, name="dtab_gs", align_bytes=64)
        nc.vector.tensor_copy(tab_gs[:], tab_s[:].indirect(offsets[:]))
        w1_q = at(B, [P, R], U32, "w1_q")
        w1_s = keep.tile([P, R], U8, name="w1_s", align_bytes=64)
        nc.vector.quantize_mx(out=w1_q[:].bitcast(FP8X4), scales=w1_s[:], in_=w1_bf[:].rearrange("p r t -> p (r t)"))

        tab_gw = keep.tile([P, J], U32, name="tab_gw", align_bytes=64)
        dtab_gw = [keep.tile([P, HALF], U32, name=f"dtab_gw{h}", tag=f"dtab_gw{h}", align_bytes=64) for h in range(2)]
        a_ps = psum.tile([P, J], F32, name="a_ps")
        ta_ps = [psum.tile([P, HALF], F32, name=f"ta_ps{h}") for h in range(2)]
        c_ps = [psum.tile([P, HALF], F32, name=f"c_ps{h}") for h in range(2)]

        nc.vector.tensor_copy(tab_gw[:], tab_w[:].bitcast(U32).indirect(offsets[:]))
        nc.tensor.matmul_mx(out=a_ps[:], lhsT=w1_q[:].bitcast(FP8X4), lhsT_scale=w1_s[:],
                            rhs=tab_gw[:].bitcast(FP8X4), rhs_scale=tab_gs[:], start=True, stop=True)

        nc.vector.tensor_copy(dtab_gs[:], dtab_s[:].indirect(offsets[:]))
        a_sb = keep.tile([P, HALF], F32, name="a_sb")
        nc.scalar.copy(out=a_sb[:], in_=a_ps[:, cols[1]])
        ogs16 = keep.tile([P, 1], F32, name="ogs16")
        nc.scalar.activation(ogs16[:], og_c[:], ACT.Copy, scale=s16[:])

        for h in range(2):
            nc.vector.tensor_copy(dtab_gw[h][:], dtab_w[:].bitcast(U32).indirect(offsets[:, grps[h]]))
            nc.tensor.matmul_mx(out=ta_ps[h][:], lhsT=w1_q[:].bitcast(FP8X4), lhsT_scale=w1_s[:],
                                rhs=dtab_gw[h][:].bitcast(FP8X4), rhs_scale=dtab_gs[4:P, cols[h]], start=True, stop=True)

        sums = keep.tile([P, 2 * G], F32, name="sums", tag="sums")
        sum_a, sum_ta = sums[:, :G], sums[:, G:]
        nc.vector.tensor_reduce(sum_a, by_group(a_ps[:]), AXIS_X, ALU.add)
        dy_bf = []

        def round_dy(h):
            dy_bf.append(keep.tile([P, HALF, PACK], BF16, name=f"dy_bf{h}", tag=f"dy_bf{h}", align_bytes=64))
            dst, src = interleave_views(dy_bf[h][:], dy_raw[h][:])
            nc.scalar.copy(out=dst, in_=src)

        round_dy(0)
        gate = keep.tile([P, G], F32, name="gate", tag="dy_raw0")
        rest = keep.tile([P, G], F32, name="rest")
        bend = keep.tile([P, G], F32, name="bend")
        slope = keep.tile([P, G], F32, name="slope")
        nc.scalar.activation(gate[:], sum_a, ACT.Sigmoid, bias=bias_c[:], scale=s16[:])
        nc.scalar.activation(bend[:], gate[:], ACT.Identity, bias=1.0, scale=-2.0)
        nc.scalar.activation(rest[:], gate[:], ACT.Identity, bias=1.0, scale=-1.0)

        wo_bf = keep.tile([P, R, PACK], BF16, name="wo_bf", align_bytes=64)
        round_dy(1)
        nc.gpsimd.tensor_scalar(wo_bf[:], wo_raw[:].rearrange("p t r -> p r t"), 1.0, 0.0, ALU.mult, ALU.add)
        codes = keep.tile([P, J + R], U32, name="codes", tag="dtab_gw1", align_bytes=64)
        dy_q, wo_q = codes[:, :J], codes[:, J:]
        wo_s = keep.tile([P, R], U8, name="wo_s", align_bytes=64)

        beta = keep.tile([P, G], F32, name="beta")
        gain = keep.tile([P, G], F32, name="gain")
        bent = keep.tile([P, J], F32, name="bent")
        for h in range(2):
            nc.vector.tensor_reduce(sum_ta[:, grps[h]], by_group(ta_ps[h][:]), AXIS_X, ALU.add)
        nc.vector.quantize_mx(out=wo_q.bitcast(FP8X4), scales=wo_s[:], in_=wo_bf[:].rearrange("p r t -> p (r t)"))
        dy_s = keep.tile([P, J], U8, name="dy_s", align_bytes=64)

        def last_layer(h):
            nc.vector.quantize_mx(out=dy_q[:, cols[h]].bitcast(FP8X4), scales=dy_s[:, cols[h]], in_=dy_bf[h][:].rearrange("p j t -> p (j t)"))
            nc.tensor.matmul_mx(out=c_ps[h][:], lhsT=wo_q.bitcast(FP8X4), lhsT_scale=wo_s[:],
                                rhs=dy_q[:, cols[h]].bitcast(FP8X4), rhs_scale=dy_s[:, cols[h]], start=True, stop=True)

        last_layer(0)
        nc.vector.scalar_tensor_tensor(slope[:], gate[:], ogs16[:], rest[:], ALU.mult, ALU.mult)
        nc.vector.scalar_tensor_tensor(beta[:], sum_ta, s16[:], bend[:], ALU.mult, ALU.mult)
        nc.vector.tensor_tensor(gain[:], sum_ta, slope[:], ALU.mult)
        nc.gpsimd.tensor_tensor(by_group(bent[:, cols[1]]), by_group(a_sb[:]), spread(beta[:, grps[1]]), ALU.mult)
        nc.vector.tensor_tensor(by_group(bent[:, cols[0]]), by_group(a_ps[:, cols[0]]), spread(beta[:, grps[0]]), ALU.mult)
        mix = [keep.tile([P, HALF], F32, name="mix0"), keep.tile([P, HALF], F32, name="mix1", tag="dy_raw1")]
        nc.vector.tensor_tensor(mix[0][:], ta_ps[0][:], bent[:, cols[0]], ALU.add)
        last_layer(1)
        nc.vector.tensor_tensor(mix[1][:], ta_ps[1][:], bent[:, cols[1]], ALU.add)

        terms = keep.tile([P, 2 * J], F32, name="terms")
        direct, prod = terms[:, :J], terms[:, J:]
        based = keep.tile([P, J], F32, name="based")
        sum_p = keep.tile([P, G], F32, name="sum_p")
        shift = keep.tile([P, G], F32, name="shift")
        result = keep.tile([P, J], F32, name="result")
        for h in range(2):
            nc.vector.tensor_tensor(by_group(direct[:, cols[h]]), by_group(c_ps[h][:]), spread(gain[:, grps[h]]), ALU.mult)
            nc.gpsimd.tensor_tensor(based[:, cols[h]], direct[:, cols[h]], base_sb[:, cols[h]], ALU.add)
            nc.vector.tensor_tensor(prod[:, cols[h]], c_ps[h][:], mix[h][:], ALU.mult)
        for h in range(2):
            nc.vector.tensor_reduce(sum_p[:, grps[h]], by_group(prod[:, cols[h]]), AXIS_X, ALU.add)
        for h in range(2):
            nc.vector.tensor_tensor(shift[:, grps[h]], sum_p[:, grps[h]], slope[:, grps[h]], ALU.mult)
        for h in range(2):
            nc.vector.tensor_tensor(by_group(result[:, cols[h]]), by_group(based[:, cols[h]]), spread(shift[:, grps[h]]), ALU.add)
            nc.sync.dma_start(out=out[:, cols[h]], in_=result[:, cols[h]])
